import numpy as np
import ml_dtypes


def mxq(x, axis, fmt="e4m3"):
    dtype, down = {"e4m3": (ml_dtypes.float8_e4m3fn, 7), "e5m2": (ml_dtypes.float8_e5m2, 14)}[fmt]
    v = np.moveaxis(np.asarray(x, np.float32).astype(ml_dtypes.bfloat16).astype(np.float64), axis, -1)
    blocks = v.reshape(v.shape[:-1] + (-1, 32))
    amax = np.abs(blocks).max(-1, keepdims=True)
    byte = np.maximum(np.where(amax > 0, np.frexp(amax)[1] - 1 + 127, 0) - down, 1)
    scale = np.exp2(byte - 127.0)
    codes = (blocks / scale).astype(np.float32).astype(dtype).astype(np.float64)
    return np.moveaxis((codes * scale).reshape(v.shape), -1, axis)


WIDE = False


def mx_kscale(k):
    if not WIDE:
        return np.ones(k)
    levels = np.array([10, -10, 5, -5, 0])
    if k % 512:
        return np.exp2(np.random.permutation(np.resize(levels, k // 32))).repeat(32)
    a = np.empty((k // 512, 16))
    for p in range(k // 512):
        a[p, :8] = np.random.permutation(np.resize(levels, 8))
        for g in range(8):
            far = levels[np.abs(levels - a[p, g]) >= 10]
            a[p, g + 8] = far[np.random.randint(len(far))]
    return np.exp2(a.ravel()).repeat(32)


def f64(x):
    return np.asarray(x).astype(np.float64)


def striped(idx):
    return np.tile(idx.reshape(-1, 16).T, (8, 1)).astype(np.uint16)


def unstriped(offs):
    return offs[:16].T.reshape(-1).astype(np.int64)


E2M1 = np.array([0.0, 0.5, 1.0, 1.5, 2.0, 3.0, 4.0, 6.0, -0.0, -0.5, -1.0, -1.5, -2.0, -3.0, -4.0, -6.0])


def pack_weight(w, fmt):
    k, n = w.shape
    w = f64(np.asarray(w, np.float32).astype(ml_dtypes.bfloat16)).reshape(k // 32, 32, n)
    amax = np.abs(w).max(1)
    if fmt == "e4m3":
        byte = np.frexp(amax)[1] - 1 + 127 - 7
    else:
        mant, ex = np.frexp(amax / 6.0)
        byte = np.where(mant > 0.5, ex, ex - 1) + 127
    byte = np.clip(np.where(amax > 0, byte, 1), 1, 254)
    scaled = (w * np.exp2(127.0 - byte)[:, None, :]).reshape(k, n).astype(np.float32)
    by_word = np.ascontiguousarray(scaled.reshape(k // 512, 128, 4, n).transpose(0, 1, 3, 2))
    if fmt == "e4m3":
        words = by_word.astype(ml_dtypes.float8_e4m3fn).view(np.uint8)
    else:
        c = by_word.astype(ml_dtypes.float4_e2m1fn).view(np.uint8) & 0xF
        words = (c[..., 0::2] | (c[..., 1::2] << 4)).reshape(k // 512, 128, 2 * n)
    return np.ascontiguousarray(words), np.ascontiguousarray(byte.astype(np.uint8).reshape(k // 512, 16, n))


def unpack_weight(words, scales, fmt):
    g, _, n = scales.shape
    words = np.ascontiguousarray(words).reshape(g, 128, n, -1)
    if fmt == "e4m3":
        vals = words.view(ml_dtypes.float8_e4m3fn).astype(np.float64)
    else:
        nib = np.empty((g, 128, n, 4), np.uint8)
        nib[..., 0::2] = words & 0xF
        nib[..., 1::2] = words >> 4
        vals = E2M1[nib]
    vals = vals * np.repeat(np.exp2(scales.astype(np.float64) - 127.0), 8, axis=1)[..., None]
    return vals.transpose(0, 1, 3, 2).reshape(g * 512, n)


def gelu(v):
    return 0.5 * v * (1.0 + np.tanh(np.sqrt(2.0 / np.pi) * (v + 0.044715 * v**3)))


def striped8(idx):
    return np.concatenate([v.reshape(-1, 16).T for v in idx]).astype(np.uint16)


def unstriped8(offs):
    return np.stack([offs[16 * g:16 * g + 16].T.reshape(-1) for g in range(8)]).astype(np.int64)


def heads(h, wgt, idx8):
    r = np.arange(h.shape[0])
    return wgt[r // 4 % 128] * h[r[:, None], idx8[r % 512 // 64]]


def put_heads(h, wgs, idx8, t2):
    r = np.arange(h.shape[0])
    page = np.zeros((h.shape[0], t2))
    page[r[:, None], idx8[r % 512 // 64]] = wgs[r // 4 % 128] * h
    return page


K, H, N, T, S, P, T2 = 1024, 1024, 512, 4096, 1024, 512, 1024

def setup_inputs():
    n = np.random.standard_normal
    s = mx_kscale(K)[:, None]
    u = mx_kscale(H)[:, None]
    d = {}
    d["tab_words"], d["tab_scales"] = pack_weight(n((K, T)) * s, "e4m3")
    d["offs"] = striped(np.random.permutation(T)[:S])
    d["w1"] = (n((K, H)) / s / K ** 0.5).astype(np.float32)
    d["gain"] = (np.exp(0.4 * n(H)) * u[:, 0]).astype(np.float32)
    d["wgt"] = np.repeat(np.random.uniform(0.5, 2.0, (8, P)), 16, axis=0).astype(np.float32)
    d["offs2"] = striped8(np.stack([np.random.permutation(S)[:P] for _ in range(8)]))
    d["base"] = (0.8 * n(H) * u[:, 0]).astype(np.float32)
    d["w2_words"], d["w2_scales"] = pack_weight(n((H, N)) / u / H ** 0.5, "e2m1")
    d["w3"] = (n((H, N)) / u / H ** 0.5).astype(np.float32)
    d["w4_words"], d["w4_scales"] = pack_weight(n((H, N)) / u / H ** 0.5, "e4m3")
    d["wgo"] = np.repeat(np.random.uniform(0.5, 2.0, (8, P)), 16, axis=0).astype(np.float32)
    d["offs3"] = striped8(np.stack([np.random.permutation(T2)[:P] for _ in range(8)]))
    return d

def reference(tab_words, tab_scales, offs, w1, gain, wgt, offs2, base, w2_words, w2_scales, w3, w4_words, w4_scales, wgo, offs3):
    v = unpack_weight(tab_words, tab_scales, "e4m3")[:, unstriped(offs)]
    h = (mxq(f64(w1), 0, "e4m3").T @ v) * f64(gain)[:, None]
    x = heads(h, f64(wgt), unstriped8(offs2)) - f64(base)[:, None]
    xq = mxq(x, 0, "e4m3")
    e1 = unpack_weight(w2_words, w2_scales, "e2m1").T @ xq
    e2 = mxq(f64(w3), 0, "e4m3").T @ xq
    e3 = unpack_weight(w4_words, w4_scales, "e4m3").T @ xq
    y = np.maximum(e1, e2) - np.minimum(e2, e3)
    return put_heads(y, f64(wgo), unstriped8(offs3), T2)

@@ -1,0 +1,250 @@
+from contextlib import ExitStack
+
+import concourse.mybir as mybir
+from concourse.masks import make_identity
+
+K, H, N, T, S, M, T2 = 1024, 1024, 512, 4096, 1024, 512, 1024
+FLOPS = 2 * K * H * S + 3 * 2 * H * N * M
+
+F32 = mybir.dt.float32
+BF16 = mybir.dt.bfloat16
+I32 = mybir.dt.int32
+U32 = mybir.dt.uint32
+U16 = mybir.dt.uint16
+U8 = mybir.dt.uint8
+E4M3 = mybir.dt.float8_e4m3fn_x4
+E2M1 = mybir.dt.float4_e2m1fn_x4
+ALU = mybir.AluOpType
+ACT = mybir.ActivationFunctionType
+
+P = 128
+PACK = 4
+PASS = P * PACK
+BANK = 512
+HALF = M // 2
+CHUNK = 256
+
+
+def tile_list_truffle_ripeness_spread_kernel(
+    tc, tab_words, tab_scales, offs, w1, gain, wgt, offs2, base,
+    w2_words, w2_scales, w3, w4_words, w4_scales, wgo, offs3, out,
+):
+    nc = tc.nc
+    with ExitStack() as ctx:
+        keep = ctx.enter_context(tc.tile_pool(name="keep", bufs=1))
+        ring = ctx.enter_context(tc.tile_pool(name="ring", bufs=2))
+        psum = ctx.enter_context(tc.psum_pool(name="psum", bufs=8))
+
+        def held(name, shape, dtype):
+            return keep.tile(shape, dtype, name=name, align_bytes=64)
+
+        def bank(name, shape):
+            return psum.tile(shape, F32, name=name, tag="bank")
+
+        idx = held("idx", [P, S // 16], U16)
+        idx2 = held("idx2", [P, M // 16], U16)
+        idx3 = held("idx3", [P, M // 16], U16)
+        tab = [held("tab%d" % a, [P, T], I32) for a in range(2)]
+        tab_sc = keep.tile([P, T], U8, name="tab_sc", tag="scales_then_words", align_bytes=64)
+        w4_sc = held("w4_sc", [P, N], U8)
+        w2_sc = held("w2_sc", [P, 2, N], U8)
+        w4_sb = held("w4_sb", [P, 2, N], I32)
+        w2_sb = held("w2_sb", [P, 2, 2 * N], U8)
+        wgt_sb = held("wgt_sb", [P, M], F32)
+        wgo_sb = held("wgo_sb", [P, M], F32)
+        gain_sb = held("gain_sb", [P, 2, PACK], F32)
+        base_sb = held("base_sb", [P, 2, PACK], F32)
+        neg_base = held("neg_base", [P, 2, PACK], F32)
+        ident = held("ident", [P, P], F32)
+        pages = [held("page%d" % i, [P, T2], F32) for i in range(PACK)]
+
+        def load_chunk(name, w, a, c0):
+            raw = held(name, [P, PACK, CHUNK], F32)
+            rows = w[a * PASS:(a + 1) * PASS, c0:c0 + CHUNK]
+            nc.sync.dma_start(out=raw[:], in_=rows.rearrange("(p j) c -> p j c", j=PACK))
+            return raw
+
+        nc.vector.memset(tab_sc[:].bitcast(I32), 0)
+        def load_table(a):
+            words = tab_words[a].rearrange("p t i -> p (t i)").bitcast(I32)
+            for c0 in range(0, T, T // 2):
+                nc.sync.dma_start(out=tab[a][:, c0:c0 + T // 2], in_=words[:, c0:c0 + T // 2])
+
+        nc.sync.dma_start(idx[:], offs)
+        load_table(0)
+        load_table(1)
+        nc.sync.dma_start(idx2[:], offs2)
+        nc.sync.dma_start(idx3[:], offs3)
+        nc.sync.dma_start(out=gain_sb[:], in_=gain.rearrange("(b p i) -> p b i", b=2, i=PACK))
+        nc.sync.dma_start(out=base_sb[:], in_=base.rearrange("(b p i) -> p b i", b=2, i=PACK))
+        for q in range(4):
+            nc.gpsimd.dma_start(out=tab_sc[32 * q:32 * q + 8, :].bitcast(I32),
+                                in_=tab_scales[:, 4 * q:4 * q + 4, :].bitcast(I32))
+        w1_raw = {}
+        for b in range(2):
+            for a in range(2):
+                for c in range(2):
+                    w1_raw[b, a, c] = load_chunk("w1_raw%d%d%d" % (b, a, c), w1, a, b * PASS + c * CHUNK)
+            if b == 0:
+                nc.sync.dma_start(out=wgt_sb[:], in_=wgt)
+        w3_raw = {}
+        for a in range(2):
+            for c in range(2):
+                w3_raw[a, c] = load_chunk("w3_raw%d%d" % (a, c), w3, a, c * CHUNK)
+        nc.sync.dma_start(out=w4_sb[:], in_=w4_words.rearrange("a p n i -> p a (n i)").bitcast(I32))
+        nc.sync.dma_start(out=w2_sb[:].bitcast(I32), in_=w2_words.rearrange("a p n -> p a n").bitcast(I32))
+        nc.sync.dma_start(out=wgo_sb[:], in_=wgo)
+        nc.vector.memset(w4_sc[:].bitcast(I32), 0)
+        nc.vector.memset(w2_sc[:].bitcast(I32), 0)
+        for q in range(4):
+            nc.sync.dma_start(out=w4_sc[32 * q:32 * q + 8, :].bitcast(I32),
+                                in_=w4_scales[:, 4 * q:4 * q + 4, :].bitcast(I32))
+            nc.sync.dma_start(out=w2_sc[32 * q:32 * q + 4, :, :].bitcast(I32),
+                                in_=w2_scales[:, 4 * q:4 * q + 4, :].rearrange("a r n -> r a n").bitcast(I32))
+        make_identity(nc, ident[:])
+        for page in pages:
+            nc.vector.memset(page[:], 0.0)
+        nc.vector.tensor_scalar_mul(neg_base[:], base_sb[:], -1.0)
+
+        v_sc = held("v_sc", [P, S], U8)
+        nc.vector.tensor_copy(v_sc[:], tab_sc[:].indirect(idx[:]))
+        v = [held("v0", [P, S], U32), keep.tile([P, S], U32, name="v1", tag="scales_then_words", align_bytes=64)]
+        for a in range(2):
+            nc.vector.tensor_copy(v[a][:], tab[a][:].bitcast(U32).indirect(idx[:]))
+
+        def copy_on(engine, dst, src):
+            if engine == "scalar":
+                nc.scalar.copy(dst, src)
+            else:
+                nc.vector.tensor_copy(dst, src)
+
+        def quantise(name, grouped, width):
+            codes = held(name + "_codes", [P, width], U32)
+            scales = held(name + "_scales", [P, width], U8)
+            nc.vector.quantize_mx(out=codes[:].bitcast(E4M3), scales=scales[:], in_=grouped)
+            return codes, scales
+
+        def prepare_w1(b, a, engines):
+            grouped = ring.tile([P, PACK, P, PACK], BF16, name="w1_grouped%d%d" % (b, a), tag="grouped", bufs=3, align_bytes=64)
+            for c in range(2):
+                cols = slice(c * CHUNK // PACK, (c + 1) * CHUNK // PACK)
+                copy_on(engines[c], grouped[:, :, cols, :].rearrange("p t m j -> p m j t"),
+                        w1_raw[b, a, c][:].rearrange("p j (m t) -> p m j t", t=PACK))
+            return quantise("w1_%d%d" % (b, a), grouped[:].rearrange("p t m j -> p (t m j)"), PASS)
+
+        def prepare_w3(a, engines):
+            grouped = ring.tile([P, N, PACK], BF16, name="w3_grouped%d" % a, tag="grouped", bufs=3, align_bytes=64)
+            for c in range(2):
+                copy_on(engines[c], grouped[:, c * CHUNK:(c + 1) * CHUNK, :].rearrange("p (c s) j -> p c j s", s=4),
+                        w3_raw[a, c][:].rearrange("p j (c s) -> p c j s", s=4))
+            return quantise("w3_%d" % a, grouped[:].rearrange("p n j -> p (n j)"), N)
+
+        def h_pass(acc, w1q, a, i, s):
+            codes, scales = w1q
+            nc.tensor.matmul_mx(
+                out=acc[:], lhsT=codes[:, i * P:(i + 1) * P].bitcast(E4M3), lhsT_scale=scales[:, i * P:(i + 1) * P],
+                rhs=v[a][:, s * BANK:(s + 1) * BANK].bitcast(E4M3), rhs_scale=v_sc[4 * a:, s * BANK:(s + 1) * BANK],
+                start=(a == 0), stop=(a == 1))
+
+        h = {}
+
+        def h_out(b, i, accs):
+            h[b, i] = held("h%d%d" % (b, i), [P, S], F32)
+            for s in range(2):
+                nc.scalar.activation(h[b, i][:, s * BANK:(s + 1) * BANK], accs[s][:], ACT.Copy, scale=gain_sb[:, b, i:i + 1])
+
+        stage = [held("picked%d" % n, [P, PACK, HALF], F32) for n in range(2)]
+        picked = {(0, 0): stage[0], (1, 0): stage[1], (0, 1): stage[1], (1, 1): stage[0]}
+        less = {}
+
+        def pick(b, half, i):
+            if i == 0:
+                less[b, half] = held("less%d%d" % (b, half), [P, PACK, HALF], BF16)
+            nc.vector.tensor_tensor(picked[b, half][:, i, :], h[b, i][:].indirect(idx2[:, 16 * half:16 * half + 16]),
+                                    wgt_sb[:, half * HALF:(half + 1) * HALF], ALU.mult)
+            nc.scalar.activation(less[b, half][:, i, :], picked[b, half][:, i, :], ACT.Identity, bias=neg_base[:, b, i:i + 1])
+
+        xq = {}
+
+        def prepare_x(b, half, engine):
+            grouped = ring.tile([P, HALF, PACK], BF16, name="x_grouped%d%d" % (b, half), tag="x_grouped", align_bytes=64)
+            copy_on(engine, grouped[:].rearrange("p (c s) i -> p c i s", s=4),
+                    less[b, half][:].rearrange("p i (c s) -> p c i s", s=4))
+            xq[b, half] = quantise("x%d%d" % (b, half), grouped[:].rearrange("p m i -> p (m i)"), HALF)
+
+        w1q = {}
+        w1q[0, 0] = prepare_w1(0, 0, ("scalar", "scalar"))
+        w1q[0, 1] = prepare_w1(0, 1, ("scalar", "vector"))
+        accs = {(i, s): bank("h_acc0%d%d" % (i, s), [P, BANK]) for i in range(PACK) for s in range(2)}
+        for i in range(PACK):
+            for s in range(2):
+                h_pass(accs[i, s], w1q[0, 0], 0, i, s)
+        for i in range(PACK):
+            for s in range(2):
+                h_pass(accs[i, s], w1q[0, 1], 1, i, s)
+            h_out(0, i, [accs[i, 0], accs[i, 1]])
+        w1q[1, 0] = prepare_w1(1, 0, ("vector", "vector"))
+        w1q[1, 1] = prepare_w1(1, 1, ("vector", "vector"))
+        for i in range(PACK):
+            pair = [bank("h_acc1%d%d" % (i, s), [P, BANK]) for s in range(2)]
+            for s in range(2):
+                for a in range(2):
+                    h_pass(pair[s], w1q[1, a], a, i, s)
+            h_out(1, i, pair)
+        for i in range(PACK):
+            pick(0, 0, i)
+        w3q = [prepare_w3(a, ("vector", "vector")) for a in range(2)]
+        for i in range(PACK):
+            pick(1, 0, i)
+        for b in range(2):
+            prepare_x(b, 0, "vector")
+
+        y = [held("y%d" % half, [P, PACK, HALF], F32) for half in range(2)]
+
+        def scores(half, q):
+            cols = slice(q * P, (q + 1) * P)
+            moving = {
+                "e2": [(w3q[a][0][:].bitcast(E4M3), w3q[a][1][:]) for a in range(2)],
+                "e3": [(w4_sb[:, a, :].bitcast(E4M3), w4_sc[4 * a:, :]) for a in range(2)],
+                "e1": [(w2_sb[:, a, :].bitcast(E2M1), w2_sc[:, a, :]) for a in range(2)],
+            }
+            turned = {}
+            for name in ("e2", "e3", "e1"):
+                acc = bank("%s_acc%d%d" % (name, half, q), [P, N])
+                for a in range(2):
+                    codes, scales = xq[a, half]
+                    nc.tensor.matmul_mx(
+                        out=acc[:], lhsT=codes[:, cols].bitcast(E4M3), lhsT_scale=scales[:, cols],
+                        rhs=moving[name][a][0], rhs_scale=moving[name][a][1], start=(a == 0), stop=(a == 1))
+                sb = ring.tile([P, PACK, P], F32, name="%s_sb%d%d" % (name, half, q), tag=name)
+                src = acc[:].rearrange("m (p i) -> m i p", i=PACK)
+                nc.scalar.activation(sb[:], src, ACT.Copy, scale=-1.0 if name == "e2" else 1.0)
+                turned[name] = sb
+            diff = {}
+            for name in ("e3", "e1"):
+                diff[name] = bank("%s_diff%d%d" % (name, half, q), [P, PACK, P])
+                for i in range(PACK):
+                    nc.tensor.matmul(diff[name][:, i, :], lhsT=turned["e2"][:, i, :], rhs=ident[:], is_transpose=True, start=True, stop=False)
+                    nc.tensor.matmul(diff[name][:, i, :], lhsT=turned[name][:, i, :], rhs=ident[:], is_transpose=True, start=False, stop=True)
+            below = ring.tile([P, PACK, P], F32, name="below%d%d" % (half, q), tag="below")
+            nc.scalar.activation(below[:], diff["e3"][:], ACT.Relu, scale=-1.0)
+            nc.vector.scalar_tensor_tensor(y[half][:, :, cols], diff["e1"][:], 0.0, below[:], ALU.max, ALU.add)
+
+        def put(half, i):
+            nc.vector.tensor_tensor(pages[i][:].indirect(idx3[:, 16 * half:16 * half + 16]), y[half][:, i, :],
+                                    wgo_sb[:, half * HALF:(half + 1) * HALF], ALU.mult)
+
+        for q in range(2):
+            scores(0, q)
+        for b in range(2):
+            for i in range(PACK):
+                pick(b, 1, i)
+            prepare_x(b, 1, ("scalar", "vector")[b])
+        for q in range(2):
+            scores(1, q)
+        for i in range(PACK):
+            put(0, i)
+        out_rows = out.rearrange("(p i) t -> i p t", i=PACK)
+        for i in range(PACK):
+            put(1, i)
+            nc.sync.dma_start(out=out_rows[i], in_=pages[i][:])

@@ -33,67 +33,64 @@ def tile_list_truffle_ripeness_spread_kernel(
     with ExitStack() as ctx:
         keep = ctx.enter_context(tc.tile_pool(name="keep", bufs=1))
         ring = ctx.enter_context(tc.tile_pool(name="ring", bufs=2))
-        psum = ctx.enter_context(tc.psum_pool(name="psum", bufs=8))
+        reused = ctx.enter_context(tc.tile_pool(name="reused", bufs=1))
+        psum = ctx.enter_context(tc.psum_pool(name="psum", bufs=1))
 
         def held(name, shape, dtype):
             return keep.tile(shape, dtype, name=name, align_bytes=64)
 
-        def bank(name, shape):
-            return psum.tile(shape, F32, name=name, tag="bank")
+        def placed(name, shape, dtype, kib):
+            return reused.tile(shape, dtype, name=name, align_bytes=64, offset=kib * 1024)
+
+        def bank(name, shape, number):
+            return psum.tile(shape, F32, name=name, offset=number * 2048)
 
         idx = held("idx", [P, S // 16], U16)
         idx2 = held("idx2", [P, M // 16], U16)
         idx3 = held("idx3", [P, M // 16], U16)
-        tab = [held("tab%d" % a, [P, T], I32) for a in range(2)]
-        tab_sc = keep.tile([P, T], U8, name="tab_sc", tag="scales_then_words", align_bytes=64)
+        tab = [placed("tab%d" % a, [P, T], I32, 16 * a) for a in range(2)]
+        tab_sc = placed("tab_sc", [P, T], U8, 32)
         w4_sc = held("w4_sc", [P, N], U8)
         w2_sc = held("w2_sc", [P, 2, N], U8)
         w4_sb = held("w4_sb", [P, 2, N], I32)
         w2_sb = held("w2_sb", [P, 2, 2 * N], U8)
         wgt_sb = held("wgt_sb", [P, M], F32)
         wgo_sb = held("wgo_sb", [P, M], F32)
-        gain_sb = held("gain_sb", [P, 2, PACK], F32)
-        base_sb = held("base_sb", [P, 2, PACK], F32)
+        gain_sb = [held("gain_sb%d" % b, [P, PACK], F32) for b in range(2)]
+        base_sb = [held("base_sb%d" % b, [P, PACK], F32) for b in range(2)]
         neg_base = held("neg_base", [P, 2, PACK], F32)
         ident = held("ident", [P, P], F32)
-        pages = [held("page%d" % i, [P, T2], F32) for i in range(PACK)]
 
-        def load_chunk(name, w, a, c0):
-            raw = held(name, [P, PACK, CHUNK], F32)
-            rows = w[a * PASS:(a + 1) * PASS, c0:c0 + CHUNK]
+        def load_rows(name, w, a, c0):
+            raw = held(name, [P, PACK, PASS], F32)
+            rows = w[a * PASS:(a + 1) * PASS, c0:c0 + PASS]
             nc.sync.dma_start(out=raw[:], in_=rows.rearrange("(p j) c -> p j c", j=PACK))
             return raw
 
-        nc.vector.memset(tab_sc[:].bitcast(I32), 0)
         def load_table(a):
-            words = tab_words[a].rearrange("p t i -> p (t i)").bitcast(I32)
-            for c0 in range(0, T, T // 2):
-                nc.sync.dma_start(out=tab[a][:, c0:c0 + T // 2], in_=words[:, c0:c0 + T // 2])
+            nc.sync.dma_start(out=tab[a][:], in_=tab_words[a].rearrange("p t i -> p (t i)").bitcast(I32))
 
-        nc.sync.dma_start(idx[:], offs)
-        load_table(0)
-        load_table(1)
-        nc.sync.dma_start(idx2[:], offs2)
-        nc.sync.dma_start(idx3[:], offs3)
-        nc.sync.dma_start(out=gain_sb[:], in_=gain.rearrange("(b p i) -> p b i", b=2, i=PACK))
-        nc.sync.dma_start(out=base_sb[:], in_=base.rearrange("(b p i) -> p b i", b=2, i=PACK))
+        nc.vector.memset(tab_sc[:].bitcast(I32), 0)
         for q in range(4):
             nc.gpsimd.dma_start(out=tab_sc[32 * q:32 * q + 8, :].bitcast(I32),
                                 in_=tab_scales[:, 4 * q:4 * q + 4, :].bitcast(I32))
         w1_raw = {}
-        for b in range(2):
-            for a in range(2):
-                for c in range(2):
-                    w1_raw[b, a, c] = load_chunk("w1_raw%d%d%d" % (b, a, c), w1, a, b * PASS + c * CHUNK)
-            if b == 0:
-                nc.sync.dma_start(out=wgt_sb[:], in_=wgt)
-        w3_raw = {}
+        nc.sync.dma_start(idx[:], offs)
+        load_table(0)
+        w1_raw[0, 0] = load_rows("w1_raw00", w1, 0, 0)
+        load_table(1)
+        nc.sync.dma_start(idx2[:], offs2)
+        nc.sync.dma_start(idx3[:], offs3)
+        for dst, src in ((gain_sb, gain), (base_sb, base)):
+            for b in range(2):
+                nc.sync.dma_start(out=dst[b][:], in_=src[b * PASS:(b + 1) * PASS].rearrange("(p i) -> p i", i=PACK))
+        w1_raw[0, 1] = load_rows("w1_raw01", w1, 1, 0)
+        nc.sync.dma_start(out=wgt_sb[:], in_=wgt)
         for a in range(2):
-            for c in range(2):
-                w3_raw[a, c] = load_chunk("w3_raw%d%d" % (a, c), w3, a, c * CHUNK)
+            w1_raw[1, a] = load_rows("w1_raw1%d" % a, w1, a, PASS)
+        w3_raw = [load_rows("w3_raw%d" % a, w3, a, 0) for a in range(2)]
         nc.sync.dma_start(out=w4_sb[:], in_=w4_words.rearrange("a p n i -> p a (n i)").bitcast(I32))
         nc.sync.dma_start(out=w2_sb[:].bitcast(I32), in_=w2_words.rearrange("a p n -> p a n").bitcast(I32))
-        nc.sync.dma_start(out=wgo_sb[:], in_=wgo)
         nc.vector.memset(w4_sc[:].bitcast(I32), 0)
         nc.vector.memset(w2_sc[:].bitcast(I32), 0)
         for q in range(4):
@@ -101,15 +98,16 @@ def tile_list_truffle_ripeness_spread_kernel(
                                 in_=w4_scales[:, 4 * q:4 * q + 4, :].bitcast(I32))
             nc.sync.dma_start(out=w2_sc[32 * q:32 * q + 4, :, :].bitcast(I32),
                                 in_=w2_scales[:, 4 * q:4 * q + 4, :].rearrange("a r n -> r a n").bitcast(I32))
+        nc.sync.dma_start(out=wgo_sb[:], in_=wgo)
         make_identity(nc, ident[:])
-        for page in pages:
-            nc.vector.memset(page[:], 0.0)
-        nc.vector.tensor_scalar_mul(neg_base[:], base_sb[:], -1.0)
+        for b in range(2):
+            nc.scalar.activation(neg_base[:, b, :], base_sb[b][:], ACT.Copy, scale=-1.0)
 
         v_sc = held("v_sc", [P, S], U8)
         nc.vector.tensor_copy(v_sc[:], tab_sc[:].indirect(idx[:]))
-        v = [held("v0", [P, S], U32), keep.tile([P, S], U32, name="v1", tag="scales_then_words", align_bytes=64)]
-        for a in range(2):
+        v = [held("v0", [P, S], U32), placed("v1", [P, S], U32, 34)]
+
+        def gather_table(a):
             nc.vector.tensor_copy(v[a][:], tab[a][:].bitcast(U32).indirect(idx[:]))
 
         def copy_on(engine, dst, src):
@@ -118,26 +116,32 @@ def tile_list_truffle_ripeness_spread_kernel(
             else:
                 nc.vector.tensor_copy(dst, src)
 
-        def quantise(name, grouped, width):
-            codes = held(name + "_codes", [P, width], U32)
-            scales = held(name + "_scales", [P, width], U8)
-            nc.vector.quantize_mx(out=codes[:].bitcast(E4M3), scales=scales[:], in_=grouped)
+        def quantise(name, grouped, widths, codes=None):
+            total = sum(widths)
+            if codes is None:
+                codes = held(name + "_codes", [P, total], U32)
+            scales = held(name + "_scales", [P, total], U8)
+            c0 = 0
+            for width in widths:
+                nc.vector.quantize_mx(out=codes[:, c0:c0 + width].bitcast(E4M3), scales=scales[:, c0:c0 + width],
+                                      in_=grouped[:, PACK * c0:PACK * (c0 + width)])
+                c0 = c0 + width
             return codes, scales
 
-        def prepare_w1(b, a, engines):
-            grouped = ring.tile([P, PACK, P, PACK], BF16, name="w1_grouped%d%d" % (b, a), tag="grouped", bufs=3, align_bytes=64)
-            for c in range(2):
-                cols = slice(c * CHUNK // PACK, (c + 1) * CHUNK // PACK)
-                copy_on(engines[c], grouped[:, :, cols, :].rearrange("p t m j -> p m j t"),
-                        w1_raw[b, a, c][:].rearrange("p j (m t) -> p m j t", t=PACK))
-            return quantise("w1_%d%d" % (b, a), grouped[:].rearrange("p t m j -> p (t m j)"), PASS)
+        def prepare_w1(b, a, on_vector, kib, widths=(PASS,), codes=None):
+            grouped = placed("w1_grouped%d%d" % (b, a), [P, PACK, P, PACK], BF16, kib)
+            dst = grouped[:].rearrange("p t m j -> p m j t")
+            src = w1_raw[b, a][:].rearrange("p j (m t) -> p m j t", t=PACK)
+            for engine, m0, m1 in (("vector", 0, on_vector), ("scalar", on_vector, P)):
+                if m1 > m0:
+                    copy_on(engine, dst[:, m0:m1], src[:, m0:m1])
+            return quantise("w1_%d%d" % (b, a), grouped[:].rearrange("p t m j -> p (t m j)"), widths, codes)
 
-        def prepare_w3(a, engines):
-            grouped = ring.tile([P, N, PACK], BF16, name="w3_grouped%d" % a, tag="grouped", bufs=3, align_bytes=64)
-            for c in range(2):
-                copy_on(engines[c], grouped[:, c * CHUNK:(c + 1) * CHUNK, :].rearrange("p (c s) j -> p c j s", s=4),
-                        w3_raw[a, c][:].rearrange("p j (c s) -> p c j s", s=4))
-            return quantise("w3_%d" % a, grouped[:].rearrange("p n j -> p (n j)"), N)
+        def prepare_w3(a, engine, kib):
+            grouped = placed("w3_grouped%d" % a, [P, N, PACK], BF16, kib)
+            copy_on(engine, grouped[:].rearrange("p (c s) j -> p c j s", s=4),
+                    w3_raw[a][:].rearrange("p j (c s) -> p c j s", s=4))
+            return quantise("w3_%d" % a, grouped[:].rearrange("p n j -> p (n j)"), (N,))
 
         def h_pass(acc, w1q, a, i, s):
             codes, scales = w1q
@@ -151,31 +155,42 @@ def tile_list_truffle_ripeness_spread_kernel(
         def h_out(b, i, accs):
             h[b, i] = held("h%d%d" % (b, i), [P, S], F32)
             for s in range(2):
-                nc.scalar.activation(h[b, i][:, s * BANK:(s + 1) * BANK], accs[s][:], ACT.Copy, scale=gain_sb[:, b, i:i + 1])
+                dst = h[b, i][:, s * BANK:(s + 1) * BANK]
+                if (b, i, s) == (0, 0, 1):
+                    nc.vector.tensor_scalar_mul(dst, accs[s][:], gain_sb[b][:, i:i + 1])
+                else:
+                    nc.scalar.activation(dst, accs[s][:], ACT.Copy, scale=gain_sb[b][:, i:i + 1])
 
-        stage = [held("picked%d" % n, [P, PACK, HALF], F32) for n in range(2)]
-        picked = {(0, 0): stage[0], (1, 0): stage[1], (0, 1): stage[1], (1, 1): stage[0]}
+        picked = {}
         less = {}
 
         def pick(b, half, i):
             if i == 0:
-                less[b, half] = held("less%d%d" % (b, half), [P, PACK, HALF], BF16)
+                shape = [P, PACK, HALF]
+                picked[b, half] = placed("picked%d1" % b, shape, F32, 40 + 4 * b) if half else held("picked%d0" % b, shape, F32)
+                less[b, half] = placed("less10", shape, BF16, 43) if (b, half) == (1, 0) else held("less%d%d" % (b, half), shape, BF16)
             nc.vector.tensor_tensor(picked[b, half][:, i, :], h[b, i][:].indirect(idx2[:, 16 * half:16 * half + 16]),
                                     wgt_sb[:, half * HALF:(half + 1) * HALF], ALU.mult)
             nc.scalar.activation(less[b, half][:, i, :], picked[b, half][:, i, :], ACT.Identity, bias=neg_base[:, b, i:i + 1])
 
         xq = {}
 
-        def prepare_x(b, half, engine):
-            grouped = ring.tile([P, HALF, PACK], BF16, name="x_grouped%d%d" % (b, half), tag="x_grouped", align_bytes=64)
-            copy_on(engine, grouped[:].rearrange("p (c s) i -> p c i s", s=4),
+        def prepare_x(b, half):
+            shape = [P, HALF, PACK]
+            grouped = placed("x_grouped%d1" % b, shape, BF16, 48 + 2 * b) if half else held("x_grouped%d0" % b, shape, BF16)
+            copy_on("scalar" if (b, half) == (0, 1) else "vector", grouped[:].rearrange("p (c s) i -> p c i s", s=4),
                     less[b, half][:].rearrange("p i (c s) -> p c i s", s=4))
-            xq[b, half] = quantise("x%d%d" % (b, half), grouped[:].rearrange("p m i -> p (m i)"), HALF)
+            xq[b, half] = quantise("x%d%d" % (b, half), grouped[:].rearrange("p m i -> p (m i)"), (HALF,))
 
         w1q = {}
-        w1q[0, 0] = prepare_w1(0, 0, ("scalar", "scalar"))
-        w1q[0, 1] = prepare_w1(0, 1, ("scalar", "vector"))
-        accs = {(i, s): bank("h_acc0%d%d" % (i, s), [P, BANK]) for i in range(PACK) for s in range(2)}
+        gather_table(0)
+        pages = [placed("page%d" % i, [P, T2], F32, 4 * i) for i in range(PACK)]
+        for page in pages:
+            nc.vector.memset(page[:], 0.0)
+        w1q[0, 0] = prepare_w1(0, 0, 0, 52, codes=placed("w1_00_codes", [P, PASS], U32, 32))
+        gather_table(1)
+        w1q[0, 1] = prepare_w1(0, 1, 88, 16, widths=(P, P, 2 * P))
+        accs = {(i, s): bank("h_acc0%d%d" % (i, s), [P, BANK], 2 * i + s) for i in range(PACK) for s in range(2)}
         for i in range(PACK):
             for s in range(2):
                 h_pass(accs[i, s], w1q[0, 0], 0, i, s)
@@ -183,68 +198,87 @@ def tile_list_truffle_ripeness_spread_kernel(
             for s in range(2):
                 h_pass(accs[i, s], w1q[0, 1], 1, i, s)
             h_out(0, i, [accs[i, 0], accs[i, 1]])
-        w1q[1, 0] = prepare_w1(1, 0, ("vector", "vector"))
-        w1q[1, 1] = prepare_w1(1, 1, ("vector", "vector"))
+        w1q[1, 0] = prepare_w1(1, 0, P, 20)
+        w1q[1, 1] = prepare_w1(1, 1, 88, 24)
         for i in range(PACK):
-            pair = [bank("h_acc1%d%d" % (i, s), [P, BANK]) for s in range(2)]
+            pair = [bank("h_acc1%d%d" % (i, s), [P, BANK], 2 * i + s) for s in range(2)]
             for s in range(2):
                 for a in range(2):
                     h_pass(pair[s], w1q[1, a], a, i, s)
             h_out(1, i, pair)
         for i in range(PACK):
             pick(0, 0, i)
-        w3q = [prepare_w3(a, ("vector", "vector")) for a in range(2)]
+        w3q = [prepare_w3(0, "scalar", 28), prepare_w3(1, "vector", 56)]
         for i in range(PACK):
             pick(1, 0, i)
         for b in range(2):
-            prepare_x(b, 0, "vector")
+            prepare_x(b, 0)
 
-        y = [held("y%d" % half, [P, PACK, HALF], F32) for half in range(2)]
+        y = {}
+
+        moving = {
+            "e2": [(w3q[a][0][:].bitcast(E4M3), w3q[a][1][:]) for a in range(2)],
+            "e3": [(w4_sb[:, a, :].bitcast(E4M3), w4_sc[4 * a:, :]) for a in range(2)],
+            "e1": [(w2_sb[:, a, :].bitcast(E2M1), w2_sc[:, a, :]) for a in range(2)],
+        }
+        score = {}
+        score_banks = {(0, 0): (0, 1, 2), (0, 1): (3, 4, 5), (1, 0): (0, 1, 2), (1, 1): (6, 7, 5)}
+
+        def score_pass(half, q, a):
+            cols = slice(q * P, (q + 1) * P)
+            codes, scales = xq[a, half]
+            for number, name in enumerate(("e2", "e3", "e1")):
+                if a == 0:
+                    score[name, half, q] = bank("%s_acc%d%d" % (name, half, q), [P, N], score_banks[half, q][number])
+                nc.tensor.matmul_mx(
+                    out=score[name, half, q][:], lhsT=codes[:, cols].bitcast(E4M3), lhsT_scale=scales[:, cols],
+                    rhs=moving[name][a][0], rhs_scale=moving[name][a][1], start=(a == 0), stop=(a == 1))
 
         def scores(half, q):
-            cols = slice(q * P, (q + 1) * P)
-            moving = {
-                "e2": [(w3q[a][0][:].bitcast(E4M3), w3q[a][1][:]) for a in range(2)],
-                "e3": [(w4_sb[:, a, :].bitcast(E4M3), w4_sc[4 * a:, :]) for a in range(2)],
-                "e1": [(w2_sb[:, a, :].bitcast(E2M1), w2_sc[:, a, :]) for a in range(2)],
-            }
             turned = {}
             for name in ("e2", "e3", "e1"):
-                acc = bank("%s_acc%d%d" % (name, half, q), [P, N])
-                for a in range(2):
-                    codes, scales = xq[a, half]
-                    nc.tensor.matmul_mx(
-                        out=acc[:], lhsT=codes[:, cols].bitcast(E4M3), lhsT_scale=scales[:, cols],
-                        rhs=moving[name][a][0], rhs_scale=moving[name][a][1], start=(a == 0), stop=(a == 1))
                 sb = ring.tile([P, PACK, P], F32, name="%s_sb%d%d" % (name, half, q), tag=name)
-                src = acc[:].rearrange("m (p i) -> m i p", i=PACK)
+                src = score[name, half, q][:].rearrange("m (p i) -> m i p", i=PACK)
                 nc.scalar.activation(sb[:], src, ACT.Copy, scale=-1.0 if name == "e2" else 1.0)
                 turned[name] = sb
             diff = {}
-            for name in ("e3", "e1"):
-                diff[name] = bank("%s_diff%d%d" % (name, half, q), [P, PACK, P])
+            for number, name in zip(score_banks[half, q], ("e3", "e1")):
+                diff[name] = bank("%s_diff%d%d" % (name, half, q), [P, PACK, P], number)
                 for i in range(PACK):
                     nc.tensor.matmul(diff[name][:, i, :], lhsT=turned["e2"][:, i, :], rhs=ident[:], is_transpose=True, start=True, stop=False)
                     nc.tensor.matmul(diff[name][:, i, :], lhsT=turned[name][:, i, :], rhs=ident[:], is_transpose=True, start=False, stop=True)
             below = ring.tile([P, PACK, P], F32, name="below%d%d" % (half, q), tag="below")
             nc.scalar.activation(below[:], diff["e3"][:], ACT.Relu, scale=-1.0)
-            nc.vector.scalar_tensor_tensor(y[half][:, :, cols], diff["e1"][:], 0.0, below[:], ALU.max, ALU.add)
+            return diff["e1"], below
 
-        def put(half, i):
-            nc.vector.tensor_tensor(pages[i][:].indirect(idx3[:, 16 * half:16 * half + 16]), y[half][:, i, :],
-                                    wgo_sb[:, half * HALF:(half + 1) * HALF], ALU.mult)
+        def spread(dst, diff, below):
+            nc.vector.scalar_tensor_tensor(dst, diff[:], 0.0, below[:], ALU.max, ALU.add)
 
-        for q in range(2):
-            scores(0, q)
+        def put(src, m0, m1, i):
+            nc.vector.tensor_tensor(pages[i][:].indirect(idx3[:, m0 // 16:m1 // 16]), src[:, i, :], wgo_sb[:, m0:m1], ALU.mult)
+
+        for a in range(2):
+            for q in range(2):
+                score_pass(0, q, a)
+        first = scores(0, 0)
         for b in range(2):
             for i in range(PACK):
                 pick(b, 1, i)
-            prepare_x(b, 1, ("scalar", "vector")[b])
+            prepare_x(b, 1)
+        y[0] = placed("y0", [P, PACK, P], F32, 49)
+        spread(y[0][:], *first)
+        y[1] = held("y1", [P, PACK, P], F32)
+        spread(y[1][:], *scores(0, 1))
+        y[2] = held("y2", [P, PACK, HALF], F32)
         for q in range(2):
-            scores(1, q)
-        for i in range(PACK):
-            put(0, i)
+            for i in range(PACK):
+                put(y[q], q * P, (q + 1) * P, i)
+        for q in range(2):
+            for a in range(2):
+                score_pass(1, q, a)
+        for q in range(2):
+            spread(y[2][:, :, q * P:(q + 1) * P], *scores(1, q))
         out_rows = out.rearrange("(p i) t -> i p t", i=PACK)
         for i in range(PACK):
-            put(1, i)
+            put(y[2], HALF, M, i)
             nc.sync.dma_start(out=out_rows[i], in_=pages[i][:])

from contextlib import ExitStack

import concourse.mybir as mybir
from concourse.masks import make_identity

K, H, N, T, S, M, T2 = 1024, 1024, 512, 4096, 1024, 512, 1024
FLOPS = 2 * K * H * S + 3 * 2 * H * N * M

F32 = mybir.dt.float32
BF16 = mybir.dt.bfloat16
I32 = mybir.dt.int32
U32 = mybir.dt.uint32
U16 = mybir.dt.uint16
U8 = mybir.dt.uint8
E4M3 = mybir.dt.float8_e4m3fn_x4
E2M1 = mybir.dt.float4_e2m1fn_x4
ALU = mybir.AluOpType
ACT = mybir.ActivationFunctionType

P = 128
PACK = 4
PASS = P * PACK
BANK = 512
HALF = M // 2
CHUNK = 256


def tile_list_truffle_ripeness_spread_kernel(
    tc, tab_words, tab_scales, offs, w1, gain, wgt, offs2, base,
    w2_words, w2_scales, w3, w4_words, w4_scales, wgo, offs3, out,
):
    nc = tc.nc
    with ExitStack() as ctx:
        keep = ctx.enter_context(tc.tile_pool(name="keep", bufs=1))
        ring = ctx.enter_context(tc.tile_pool(name="ring", bufs=2))
        reused = ctx.enter_context(tc.tile_pool(name="reused", bufs=1))
        psum = ctx.enter_context(tc.psum_pool(name="psum", bufs=1))

        def held(name, shape, dtype):
            return keep.tile(shape, dtype, name=name, align_bytes=64)

        def placed(name, shape, dtype, kib):
            return reused.tile(shape, dtype, name=name, align_bytes=64, offset=kib * 1024)

        def bank(name, shape, number):
            return psum.tile(shape, F32, name=name, offset=number * 2048)

        idx = held("idx", [P, S // 16], U16)
        idx2 = held("idx2", [P, M // 16], U16)
        idx3 = held("idx3", [P, M // 16], U16)
        tab = [placed("tab%d" % a, [P, T], I32, 16 * a) for a in range(2)]
        tab_sc = placed("tab_sc", [P, T], U8, 32)
        w4_sc = held("w4_sc", [P, N], U8)
        w2_sc = held("w2_sc", [P, 2, N], U8)
        w4_sb = held("w4_sb", [P, 2, N], I32)
        w2_sb = held("w2_sb", [P, 2, 2 * N], U8)
        wgt_sb = held("wgt_sb", [P, M], F32)
        wgo_sb = held("wgo_sb", [P, M], F32)
        gain_sb = [held("gain_sb%d" % b, [P, PACK], F32) for b in range(2)]
        base_sb = [held("base_sb%d" % b, [P, PACK], F32) for b in range(2)]
        neg_base = held("neg_base", [P, 2, PACK], F32)
        ident = held("ident", [P, P], F32)

        def load_rows(name, w, a, c0):
            raw = held(name, [P, PACK, PASS], F32)
            rows = w[a * PASS:(a + 1) * PASS, c0:c0 + PASS]
            nc.sync.dma_start(out=raw[:], in_=rows.rearrange("(p j) c -> p j c", j=PACK))
            return raw

        def load_table(a):
            nc.sync.dma_start(out=tab[a][:], in_=tab_words[a].rearrange("p t i -> p (t i)").bitcast(I32))

        nc.vector.memset(tab_sc[:].bitcast(I32), 0)
        for q in range(4):
            nc.gpsimd.dma_start(out=tab_sc[32 * q:32 * q + 8, :].bitcast(I32),
                                in_=tab_scales[:, 4 * q:4 * q + 4, :].bitcast(I32))
        w1_raw = {}
        nc.sync.dma_start(idx[:], offs)
        load_table(0)
        w1_raw[0, 0] = load_rows("w1_raw00", w1, 0, 0)
        load_table(1)
        nc.sync.dma_start(idx2[:], offs2)
        nc.sync.dma_start(idx3[:], offs3)
        for dst, src in ((gain_sb, gain), (base_sb, base)):
            for b in range(2):
                nc.sync.dma_start(out=dst[b][:], in_=src[b * PASS:(b + 1) * PASS].rearrange("(p i) -> p i", i=PACK))
        w1_raw[0, 1] = load_rows("w1_raw01", w1, 1, 0)
        nc.sync.dma_start(out=wgt_sb[:], in_=wgt)
        for a in range(2):
            w1_raw[1, a] = load_rows("w1_raw1%d" % a, w1, a, PASS)
        w3_raw = [load_rows("w3_raw%d" % a, w3, a, 0) for a in range(2)]
        nc.sync.dma_start(out=w4_sb[:], in_=w4_words.rearrange("a p n i -> p a (n i)").bitcast(I32))
        nc.sync.dma_start(out=w2_sb[:].bitcast(I32), in_=w2_words.rearrange("a p n -> p a n").bitcast(I32))
        nc.vector.memset(w4_sc[:].bitcast(I32), 0)
        nc.vector.memset(w2_sc[:].bitcast(I32), 0)
        for q in range(4):
            nc.sync.dma_start(out=w4_sc[32 * q:32 * q + 8, :].bitcast(I32),
                                in_=w4_scales[:, 4 * q:4 * q + 4, :].bitcast(I32))
            nc.sync.dma_start(out=w2_sc[32 * q:32 * q + 4, :, :].bitcast(I32),
                                in_=w2_scales[:, 4 * q:4 * q + 4, :].rearrange("a r n -> r a n").bitcast(I32))
        nc.sync.dma_start(out=wgo_sb[:], in_=wgo)
        make_identity(nc, ident[:])
        for b in range(2):
            nc.scalar.activation(neg_base[:, b, :], base_sb[b][:], ACT.Copy, scale=-1.0)

        v_sc = held("v_sc", [P, S], U8)
        nc.vector.tensor_copy(v_sc[:], tab_sc[:].indirect(idx[:]))
        v = [held("v0", [P, S], U32), placed("v1", [P, S], U32, 34)]

        def gather_table(a):
            nc.vector.tensor_copy(v[a][:], tab[a][:].bitcast(U32).indirect(idx[:]))

        def copy_on(engine, dst, src):
            if engine == "scalar":
                nc.scalar.copy(dst, src)
            else:
                nc.vector.tensor_copy(dst, src)

        def quantise(name, grouped, widths, codes=None):
            total = sum(widths)
            if codes is None:
                codes = held(name + "_codes", [P, total], U32)
            scales = held(name + "_scales", [P, total], U8)
            c0 = 0
            for width in widths:
                nc.vector.quantize_mx(out=codes[:, c0:c0 + width].bitcast(E4M3), scales=scales[:, c0:c0 + width],
                                      in_=grouped[:, PACK * c0:PACK * (c0 + width)])
                c0 = c0 + width
            return codes, scales

        def prepare_w1(b, a, on_vector, kib, widths=(PASS,), codes=None):
            grouped = placed("w1_grouped%d%d" % (b, a), [P, PACK, P, PACK], BF16, kib)
            dst = grouped[:].rearrange("p t m j -> p m j t")
            src = w1_raw[b, a][:].rearrange("p j (m t) -> p m j t", t=PACK)
            for engine, m0, m1 in (("vector", 0, on_vector), ("scalar", on_vector, P)):
                if m1 > m0:
                    copy_on(engine, dst[:, m0:m1], src[:, m0:m1])
            return quantise("w1_%d%d" % (b, a), grouped[:].rearrange("p t m j -> p (t m j)"), widths, codes)

        def prepare_w3(a, engine, kib):
            grouped = placed("w3_grouped%d" % a, [P, N, PACK], BF16, kib)
            copy_on(engine, grouped[:].rearrange("p (c s) j -> p c j s", s=4),
                    w3_raw[a][:].rearrange("p j (c s) -> p c j s", s=4))
            return quantise("w3_%d" % a, grouped[:].rearrange("p n j -> p (n j)"), (N,))

        def h_pass(acc, w1q, a, i, s):
            codes, scales = w1q
            nc.tensor.matmul_mx(
                out=acc[:], lhsT=codes[:, i * P:(i + 1) * P].bitcast(E4M3), lhsT_scale=scales[:, i * P:(i + 1) * P],
                rhs=v[a][:, s * BANK:(s + 1) * BANK].bitcast(E4M3), rhs_scale=v_sc[4 * a:, s * BANK:(s + 1) * BANK],
                start=(a == 0), stop=(a == 1))

        h = {}

        def h_out(b, i, accs):
            h[b, i] = held("h%d%d" % (b, i), [P, S], F32)
            for s in range(2):
                dst = h[b, i][:, s * BANK:(s + 1) * BANK]
                if (b, i, s) == (0, 0, 1):
                    nc.vector.tensor_scalar_mul(dst, accs[s][:], gain_sb[b][:, i:i + 1])
                else:
                    nc.scalar.activation(dst, accs[s][:], ACT.Copy, scale=gain_sb[b][:, i:i + 1])

        picked = {}
        less = {}

        def pick(b, half, i):
            if i == 0:
                shape = [P, PACK, HALF]
                picked[b, half] = placed("picked%d1" % b, shape, F32, 40 + 4 * b) if half else held("picked%d0" % b, shape, F32)
                less[b, half] = placed("less10", shape, BF16, 43) if (b, half) == (1, 0) else held("less%d%d" % (b, half), shape, BF16)
            nc.vector.tensor_tensor(picked[b, half][:, i, :], h[b, i][:].indirect(idx2[:, 16 * half:16 * half + 16]),
                                    wgt_sb[:, half * HALF:(half + 1) * HALF], ALU.mult)
            nc.scalar.activation(less[b, half][:, i, :], picked[b, half][:, i, :], ACT.Identity, bias=neg_base[:, b, i:i + 1])

        xq = {}

        def prepare_x(b, half):
            shape = [P, HALF, PACK]
            grouped = placed("x_grouped%d1" % b, shape, BF16, 48 + 2 * b) if half else held("x_grouped%d0" % b, shape, BF16)
            copy_on("scalar" if (b, half) == (0, 1) else "vector", grouped[:].rearrange("p (c s) i -> p c i s", s=4),
                    less[b, half][:].rearrange("p i (c s) -> p c i s", s=4))
            xq[b, half] = quantise("x%d%d" % (b, half), grouped[:].rearrange("p m i -> p (m i)"), (HALF,))

        w1q = {}
        gather_table(0)
        pages = [placed("page%d" % i, [P, T2], F32, 4 * i) for i in range(PACK)]
        for page in pages:
            nc.vector.memset(page[:], 0.0)
        w1q[0, 0] = prepare_w1(0, 0, 0, 52, codes=placed("w1_00_codes", [P, PASS], U32, 32))
        gather_table(1)
        w1q[0, 1] = prepare_w1(0, 1, 88, 16, widths=(P, P, 2 * P))
        accs = {(i, s): bank("h_acc0%d%d" % (i, s), [P, BANK], 2 * i + s) for i in range(PACK) for s in range(2)}
        for i in range(PACK):
            for s in range(2):
                h_pass(accs[i, s], w1q[0, 0], 0, i, s)
        for i in range(PACK):
            for s in range(2):
                h_pass(accs[i, s], w1q[0, 1], 1, i, s)
            h_out(0, i, [accs[i, 0], accs[i, 1]])
        w1q[1, 0] = prepare_w1(1, 0, P, 20)
        w1q[1, 1] = prepare_w1(1, 1, 88, 24)
        for i in range(PACK):
            pair = [bank("h_acc1%d%d" % (i, s), [P, BANK], 2 * i + s) for s in range(2)]
            for s in range(2):
                for a in range(2):
                    h_pass(pair[s], w1q[1, a], a, i, s)
            h_out(1, i, pair)
        for i in range(PACK):
            pick(0, 0, i)
        w3q = [prepare_w3(0, "scalar", 28), prepare_w3(1, "vector", 56)]
        for i in range(PACK):
            pick(1, 0, i)
        for b in range(2):
            prepare_x(b, 0)

        y = {}

        moving = {
            "e2": [(w3q[a][0][:].bitcast(E4M3), w3q[a][1][:]) for a in range(2)],
            "e3": [(w4_sb[:, a, :].bitcast(E4M3), w4_sc[4 * a:, :]) for a in range(2)],
            "e1": [(w2_sb[:, a, :].bitcast(E2M1), w2_sc[:, a, :]) for a in range(2)],
        }
        score = {}
        score_banks = {(0, 0): (0, 1, 2), (0, 1): (3, 4, 5), (1, 0): (0, 1, 2), (1, 1): (6, 7, 5)}

        def score_pass(half, q, a):
            cols = slice(q * P, (q + 1) * P)
            codes, scales = xq[a, half]
            for number, name in enumerate(("e2", "e3", "e1")):
                if a == 0:
                    score[name, half, q] = bank("%s_acc%d%d" % (name, half, q), [P, N], score_banks[half, q][number])
                nc.tensor.matmul_mx(
                    out=score[name, half, q][:], lhsT=codes[:, cols].bitcast(E4M3), lhsT_scale=scales[:, cols],
                    rhs=moving[name][a][0], rhs_scale=moving[name][a][1], start=(a == 0), stop=(a == 1))

        def scores(half, q):
            turned = {}
            for name in ("e2", "e3", "e1"):
                sb = ring.tile([P, PACK, P], F32, name="%s_sb%d%d" % (name, half, q), tag=name)
                src = score[name, half, q][:].rearrange("m (p i) -> m i p", i=PACK)
                nc.scalar.activation(sb[:], src, ACT.Copy, scale=-1.0 if name == "e2" else 1.0)
                turned[name] = sb
            diff = {}
            for number, name in zip(score_banks[half, q], ("e3", "e1")):
                diff[name] = bank("%s_diff%d%d" % (name, half, q), [P, PACK, P], number)
                for i in range(PACK):
                    nc.tensor.matmul(diff[name][:, i, :], lhsT=turned["e2"][:, i, :], rhs=ident[:], is_transpose=True, start=True, stop=False)
                    nc.tensor.matmul(diff[name][:, i, :], lhsT=turned[name][:, i, :], rhs=ident[:], is_transpose=True, start=False, stop=True)
            below = ring.tile([P, PACK, P], F32, name="below%d%d" % (half, q), tag="below")
            nc.scalar.activation(below[:], diff["e3"][:], ACT.Relu, scale=-1.0)
            return diff["e1"], below

        def spread(dst, diff, below):
            nc.vector.scalar_tensor_tensor(dst, diff[:], 0.0, below[:], ALU.max, ALU.add)

        def put(src, m0, m1, i):
            nc.vector.tensor_tensor(pages[i][:].indirect(idx3[:, m0 // 16:m1 // 16]), src[:, i, :], wgo_sb[:, m0:m1], ALU.mult)

        for a in range(2):
            for q in range(2):
                score_pass(0, q, a)
        first = scores(0, 0)
        for b in range(2):
            for i in range(PACK):
                pick(b, 1, i)
            prepare_x(b, 1)
        y[0] = placed("y0", [P, PACK, P], F32, 49)
        spread(y[0][:], *first)
        y[1] = held("y1", [P, PACK, P], F32)
        spread(y[1][:], *scores(0, 1))
        y[2] = held("y2", [P, PACK, HALF], F32)
        for q in range(2):
            for i in range(PACK):
                put(y[q], q * P, (q + 1) * P, i)
        for q in range(2):
            for a in range(2):
                score_pass(1, q, a)
        for q in range(2):
            spread(y[2][:, :, q * P:(q + 1) * P], *scores(1, q))
        out_rows = out.rearrange("(p i) t -> i p t", i=PACK)
        for i in range(PACK):
            put(y[2], HALF, M, i)
            nc.sync.dma_start(out=out_rows[i], in_=pages[i][:])
